import numpy as np
import ml_dtypes


def mxq(x, axis, fmt="e4m3"):
    dtype, down = {"e4m3": (ml_dtypes.float8_e4m3fn, 7), "e5m2": (ml_dtypes.float8_e5m2, 14)}[fmt]
    v = np.moveaxis(np.asarray(x, np.float32).astype(ml_dtypes.bfloat16).astype(np.float64), axis, -1)
    blocks = v.reshape(v.shape[:-1] + (-1, 32))
    amax = np.abs(blocks).max(-1, keepdims=True)
    byte = np.maximum(np.where(amax > 0, np.frexp(amax)[1] - 1 + 127, 0) - down, 1)
    scale = np.exp2(byte - 127.0)
    codes = (blocks / scale).astype(np.float32).astype(dtype).astype(np.float64)
    return np.moveaxis((codes * scale).reshape(v.shape), -1, axis)


WIDE = False


def mx_kscale(k):
    if not WIDE:
        return np.ones(k)
    levels = np.array([30, -30])
    if k % 512:
        return np.exp2(np.random.permutation(np.resize(levels, k // 32))).repeat(32)
    a = np.empty((k // 512, 16))
    for p in range(k // 512):
        a[p, :8] = np.random.permutation(np.resize(levels, 8))
        for g in range(8):
            far = levels[np.abs(levels - a[p, g]) >= 10]
            a[p, g + 8] = far[np.random.randint(len(far))]
    return np.exp2(a.ravel()).repeat(32)


def f64(x):
    return np.asarray(x).astype(np.float64)


def striped(idx):
    return np.tile(np.asarray(idx).reshape(-1, 16).T, (8, 1)).astype(np.uint16)


def unstriped(offs):
    return offs[:16].T.reshape(-1).astype(np.int64)


E2M1 = np.array([0.0, 0.5, 1.0, 1.5, 2.0, 3.0, 4.0, 6.0, -0.0, -0.5, -1.0, -1.5, -2.0, -3.0, -4.0, -6.0])


def pack_weight(w, fmt):
    k, n = w.shape
    w = f64(np.asarray(w, np.float32).astype(ml_dtypes.bfloat16)).reshape(k // 32, 32, n)
    amax = np.abs(w).max(1)
    if fmt in ("e4m3", "e5m2"):
        byte = np.frexp(amax)[1] - 1 + 127 - (7 if fmt == "e4m3" else 14)
    else:
        mant, ex = np.frexp(amax / 6.0)
        byte = np.where(mant > 0.5, ex, ex - 1) + 127
    byte = np.clip(np.where(amax > 0, byte, 1), 1, 254)
    scaled = (w * np.exp2(127.0 - byte)[:, None, :]).reshape(k, n).astype(np.float32)
    by_word = np.ascontiguousarray(scaled.reshape(k // 512, 128, 4, n).transpose(0, 1, 3, 2))
    if fmt in ("e4m3", "e5m2"):
        words = by_word.astype(ml_dtypes.float8_e4m3fn if fmt == "e4m3" else ml_dtypes.float8_e5m2).view(np.uint8)
    else:
        c = by_word.astype(ml_dtypes.float4_e2m1fn).view(np.uint8) & 0xF
        words = (c[..., 0::2] | (c[..., 1::2] << 4)).reshape(k // 512, 128, 2 * n)
    return np.ascontiguousarray(words), np.ascontiguousarray(byte.astype(np.uint8).reshape(k // 512, 16, n))


def unpack_weight(words, scales, fmt):
    g, _, n = scales.shape
    words = np.ascontiguousarray(words).reshape(g, 128, n, -1)
    if fmt in ("e4m3", "e5m2"):
        vals = words.view(ml_dtypes.float8_e4m3fn if fmt == "e4m3" else ml_dtypes.float8_e5m2).astype(np.float64)
    else:
        nib = np.empty((g, 128, n, 4), np.uint8)
        nib[..., 0::2] = words & 0xF
        nib[..., 1::2] = words >> 4
        vals = E2M1[nib]
    vals = vals * np.repeat(np.exp2(scales.astype(np.float64) - 127.0), 8, axis=1)[..., None]
    return vals.transpose(0, 1, 3, 2).reshape(g * 512, n)


K, F, T, Z, J, R, O, N, L = 512, 512, 1024, 1024, 256, 512, 128, 256, 512


def setup_inputs():
    n = np.random.standard_normal
    idx = np.random.permutation(T)[:J]
    idx2 = np.random.permutation(Z)[:J]
    idx3 = np.random.permutation(J)[:O]
    idx4 = np.random.permutation(J)[:O]
    fk = mx_kscale(K)
    fr = mx_kscale(R)
    ff = mx_kscale(F)
    fl = mx_kscale(L)
    xtp = pack_weight(n((K, T)) / fk[:, None], "e2m1")
    wp = pack_weight(n((K, R)) * 1 / np.sqrt(K) * fk[:, None] * fr, "e5m2")
    xop = pack_weight(n((F, Z)) / ff[:, None], "e5m2")
    w2p = pack_weight(n((F, R)) * 1 / np.sqrt(F) * ff[:, None] * fr, "e4m3")
    wbp = pack_weight(n((R, N)) * 1 / np.sqrt(R) / fr[:, None], "e4m3")
    sxp = pack_weight(n((L, O)) / fl[:, None], "e5m2")
    wsp = pack_weight(n((L, N)) * 1 / np.sqrt(L) * fl[:, None], "e4m3")
    return {
        "xt_words": xtp[0],
        "xt_scales": xtp[1],
        "w_words": wp[0],
        "w_scales": wp[1],
        "xo_words": xop[0],
        "xo_scales": xop[1],
        "w2_words": w2p[0],
        "w2_scales": w2p[1],
        "wb_words": wbp[0],
        "wb_scales": wbp[1],
        "sx_words": sxp[0],
        "sx_scales": sxp[1],
        "ws_words": wsp[0],
        "ws_scales": wsp[1],
        "offs": striped(idx),
        "offs2": striped(idx2),
        "offs3": striped(idx3),
        "offs4": striped(idx4),
    }


def reference(xt_words, xt_scales, w_words, w_scales, xo_words, xo_scales, w2_words, w2_scales, wb_words, wb_scales, sx_words, sx_scales, ws_words, ws_scales, offs, offs2, offs3, offs4):
    idx = unstriped(offs)
    idx2 = unstriped(offs2)
    idx3 = unstriped(offs3)
    idx4 = unstriped(offs4)
    xtu = unpack_weight(xt_words, xt_scales, "e2m1")
    wu = unpack_weight(w_words, w_scales, "e5m2")
    xou = unpack_weight(xo_words, xo_scales, "e5m2")
    w2u = unpack_weight(w2_words, w2_scales, "e4m3")
    wbu = unpack_weight(wb_words, wb_scales, "e4m3")
    sxu = unpack_weight(sx_words, sx_scales, "e5m2")
    wsu = unpack_weight(ws_words, ws_scales, "e4m3")
    xtidxg = xtu[:, idx]
    a = wu.T @ xtidxg
    xoidx2g = xou[:, idx2]
    b = w2u.T @ xoidx2g
    hid = np.maximum(a[:, idx3], b[:, idx4])
    hidq = mxq(hid, 0, "e5m2")
    y = wbu.T @ hidq + wsu.T @ sxu
    return y

@@ -1,0 +1,158 @@
+from contextlib import ExitStack
+
+import concourse.mybir as mybir
+
+F32 = mybir.dt.float32
+BF16 = mybir.dt.bfloat16
+I32 = mybir.dt.int32
+U32 = mybir.dt.uint32
+U16 = mybir.dt.uint16
+U8 = mybir.dt.uint8
+E4M3 = mybir.dt.float8_e4m3fn_x4
+E5M2 = mybir.dt.float8_e5m2_x4
+E2M1 = mybir.dt.float4_e2m1fn_x4
+COPY = mybir.ActivationFunctionType.Copy
+
+P = 128
+PACK = 4
+T, Z, J, R, O, N = 1024, 1024, 256, 512, 128, 256
+FLOPS = 335544320
+
+
+def tile_list_twotab_looked_skip_plain_kernel(
+    tc, xt_words, xt_scales, w_words, w_scales, xo_words, xo_scales, w2_words, w2_scales,
+    wb_words, wb_scales, sx_words, sx_scales, ws_words, ws_scales, offs, offs2, offs3, offs4, out,
+):
+    nc = tc.nc
+    with ExitStack() as ctx:
+        sb = ctx.enter_context(tc.tile_pool(name="sb", bufs=1))
+        ps = ctx.enter_context(tc.psum_pool(name="ps", bufs=1))
+
+        def load_list(src, name):
+            t = sb.tile(list(src.shape), U16, name=name)
+            nc.sync.dma_start(t[:], src)
+            return t
+
+        def fill_words(eng, dst, src):
+            eng.dma_start(dst.bitcast(I32), src[0].rearrange("p n t -> p (n t)").bitcast(I32))
+
+        def load_words(eng, src, cols, name, tag=""):
+            t = sb.tile([P, cols], U32, name=name, tag=tag, align_bytes=64)
+            fill_words(eng, t[:], src)
+            return t
+
+        def zeroed(eng, cols, name, tag=""):
+            t = sb.tile([P, cols], U8, name=name, tag=tag, align_bytes=64)
+            eng.memset(t[:].bitcast(I32), 0)
+            return t
+
+        def load_scales(eng, plane, src):
+            for q in range(4):
+                eng.dma_start(plane[32 * q:32 * q + 4, :].bitcast(I32), src[0].bitcast(I32)[4 * q:4 * q + 4, :])
+
+        xt_s = zeroed(nc.vector, T, "xt_s")
+        w_s = zeroed(nc.vector, R, "w_s")
+        xo_s = zeroed(nc.vector, Z, "xo_s")
+        w2_s = zeroed(nc.vector, R, "w2_s")
+
+        l1 = load_list(offs, "l1")
+        xt_w = sb.tile([P, T], U16, name="xt_w", align_bytes=64)
+        nc.sync.dma_start(xt_w[:].bitcast(I32), xt_words[0].bitcast(I32))
+        l2 = load_list(offs2, "l2")
+        load_scales(nc.sync, xt_s, xt_scales)
+        w_w = load_words(nc.sync, w_words, R, "w_w")
+        xo_w = load_words(nc.gpsimd, xo_words, Z, "xo_w")
+        w2_w = load_words(nc.gpsimd, w2_words, R, "w2_w")
+        load_scales(nc.sync, w_s, w_scales)
+        load_scales(nc.sync, xo_s, xo_scales)
+        load_scales(nc.sync, w2_s, w2_scales)
+        l3 = load_list(offs3, "l3")
+        l4 = load_list(offs4, "l4")
+
+        def gather(window, lst, dtype, cols, name, tag=""):
+            t = sb.tile([P, cols], dtype, name=name, tag=tag, align_bytes=64)
+            nc.vector.tensor_copy(t[:], window[:].indirect(lst[:]))
+            return t
+
+        def deal(src, dtype, view, name, tag=""):
+            t = sb.tile([P, R], dtype, name=name, tag=tag, align_bytes=64)
+            nc.vector.tensor_copy(t[:].bitcast(view).rearrange("p (t m) -> p t m", t=PACK),
+                                  src[:].bitcast(view).rearrange("p (m t) -> p t m", t=PACK))
+            return t
+
+        xt_wg = gather(xt_w, l1, U16, J, "xt_wg")
+        xt_sg = gather(xt_s, l1, U8, J, "xt_sg")
+        w_wd = sb.tile([P, R], U32, name="w_wd", align_bytes=64)
+        nc.scalar.copy(w_wd[:].rearrange("p (t m) -> p t m", t=PACK), w_w[:].rearrange("p (m t) -> p t m", t=PACK))
+        w_sd = deal(w_s, U8, U8, "w_sd", tag="xt_s")
+        late_w = sb.tile([P, N + O + N], U32, name="late_w", tag="w_w", align_bytes=64)
+        ws_w, sx_w, wb_w = late_w[:, 0:N], late_w[:, N:N + O], late_w[:, N + O:]
+        late_s = zeroed(nc.gpsimd, N + O + N, "late_s")
+        ws_s, sx_s, wb_s = late_s[:, 0:N], late_s[:, N:N + O], late_s[:, N + O:]
+        fill_words(nc.sync, ws_w, ws_words)
+        fill_words(nc.sync, sx_w, sx_words)
+        fill_words(nc.sync, wb_w, wb_words)
+        load_scales(nc.sync, ws_s, ws_scales)
+        load_scales(nc.sync, sx_s, sx_scales)
+        load_scales(nc.sync, wb_s, wb_scales)
+        xo_wg = gather(xo_w, l2, U32, J, "xo_wg", tag="w_s")
+        xo_sg = gather(xo_s, l2, U8, J, "xo_sg")
+        w2_wd = deal(w2_w, U32, I32, "w2_wd", tag="xo_w")
+        w2_sd = deal(w2_s, U8, U8, "w2_sd", tag="w2_w")
+
+        a_ps = [ps.tile([P, J], F32, name="a_ps%d" % t) for t in range(PACK)]
+        b_ps = [ps.tile([P, J], F32, name="b_ps%d" % t) for t in range(PACK)]
+
+        ag = sb.tile([P, PACK, O], F32, name="ag")
+        bg = sb.tile([P, PACK, O], F32, name="bg")
+        for t in range(PACK):
+            cols = slice(t * P, (t + 1) * P)
+            nc.tensor.matmul_mx(out=a_ps[t][:], lhsT=w_wd[:, cols].bitcast(E5M2), lhsT_scale=w_sd[:, cols],
+                                rhs=xt_wg[:].bitcast(E2M1), rhs_scale=xt_sg[:], start=True, stop=True)
+        a_sb = [sb.tile([P, J], F32, name="a_sb%d" % t) for t in range(PACK)]
+        for t in range(PACK):
+            nc.scalar.activation(a_sb[t][:], a_ps[t][:], COPY)
+        for t in range(PACK):
+            nc.scalar.activation(ag[:, t, :], a_sb[t][:].indirect(l3[:]), COPY)
+
+        for t in range(PACK):
+            cols = slice(t * P, (t + 1) * P)
+            nc.tensor.matmul_mx(out=b_ps[t][:], lhsT=w2_wd[:, cols].bitcast(E4M3), lhsT_scale=w2_sd[:, cols],
+                                rhs=xo_wg[:].bitcast(E5M2), rhs_scale=xo_sg[:], start=True, stop=True)
+        b_sb = [sb.tile([P, J], F32, name="b_sb%d" % t) for t in range(PACK)]
+        for t in range(PACK):
+            if t < 3:
+                nc.vector.tensor_copy(b_sb[t][:], b_ps[t][:])
+            else:
+                nc.scalar.activation(b_sb[t][:], b_ps[t][:], COPY)
+        for t in range(PACK):
+            if t < 2:
+                nc.vector.tensor_copy(bg[:, t, :], b_sb[t][:].indirect(l4[:]))
+            else:
+                nc.scalar.activation(bg[:, t, :], b_sb[t][:].indirect(l4[:]), COPY)
+
+
+        y_ps = [ps.tile([P, O], F32, name="y_ps%d" % h, tag="b_ps%d" % h) for h in range(2)]
+        for h in range(2):
+            cols = slice(h * P, (h + 1) * P)
+            nc.tensor.matmul_mx(out=y_ps[h][:], lhsT=ws_w[:, cols].bitcast(E4M3), lhsT_scale=ws_s[:, cols],
+                                rhs=sx_w.bitcast(E5M2), rhs_scale=sx_s, start=True, stop=False)
+
+        hid = sb.tile([P, O, PACK], BF16, name="hid", align_bytes=64)
+        for u in range(2):
+            pair = slice(2 * u, 2 * u + 2)
+            nc.vector.tensor_max(hid[:, :, pair], ag[:, pair, :].rearrange("p t o -> p o t"), bg[:, pair, :].rearrange("p t o -> p o t"))
+        h_w = sb.tile([P, O], U32, name="h_w", align_bytes=64)
+        h_s = sb.tile([P, O], U8, name="h_s", align_bytes=64)
+        nc.vector.quantize_mx(out=h_w[:].bitcast(E5M2), scales=h_s[:], in_=hid[:].rearrange("p o t -> p (o t)"))
+
+        for h in range(2):
+            cols = slice(h * P, (h + 1) * P)
+            nc.tensor.matmul_mx(out=y_ps[h][:], lhsT=wb_w[:, cols].bitcast(E4M3), lhsT_scale=wb_s[:, cols],
+                                rhs=h_w[:].bitcast(E5M2), rhs_scale=h_s[:], start=False, stop=True)
+        y0 = sb.tile([P, O], F32, name="y0")
+        y1 = sb.tile([P, O], F32, name="y1")
+        nc.vector.tensor_copy(y0[:], y_ps[0][:])
+        nc.sync.dma_start(out[0:P, :], y0[:])
+        nc.scalar.activation(y1[:], y_ps[1][:], COPY)
+        nc.scalar.dma_start(out[P:2 * P, :], y1[:])

@@ -68,6 +68,14 @@ def tile_list_twotab_looked_skip_plain_kernel(
         load_scales(nc.sync, w2_s, w2_scales)
         l3 = load_list(offs3, "l3")
         l4 = load_list(offs4, "l4")
+        late_s = zeroed(nc.vector, N + O + N, "late_s")
+        ws_s, sx_s, wb_s = late_s[:, 0:N], late_s[:, N:N + O], late_s[:, N + O:]
+        ws_w = load_words(nc.sync, ws_words, N, "ws_w")
+        sx_w = load_words(nc.sync, sx_words, O, "sx_w")[:]
+        load_scales(nc.sync, ws_s, ws_scales)
+        load_scales(nc.sync, sx_s, sx_scales)
+        wb_w = load_words(nc.sync, wb_words, N, "wb_w")
+        load_scales(nc.sync, wb_s, wb_scales)
 
         def gather(window, lst, dtype, cols, name, tag=""):
             t = sb.tile([P, cols], dtype, name=name, tag=tag, align_bytes=64)
@@ -80,25 +88,24 @@ def tile_list_twotab_looked_skip_plain_kernel(
                                   src[:].bitcast(view).rearrange("p (m t) -> p t m", t=PACK))
             return t
 
+        def deal_scales(src, name, tag):
+            dealt = sb.tile([P, R], U8, name=name, tag=tag, align_bytes=64)
+            for u in range(2):
+                nc.vector.tensor_copy(dealt[:].rearrange("p (t m) -> p t m", t=PACK)[:, 2 * u:2 * u + 2, :],
+                                      src[:].rearrange("p (m t) -> p t m", t=PACK)[:, 2 * u:2 * u + 2, :])
+            return dealt
+
         xt_wg = gather(xt_w, l1, U16, J, "xt_wg")
         xt_sg = gather(xt_s, l1, U8, J, "xt_sg")
         w_wd = sb.tile([P, R], U32, name="w_wd", align_bytes=64)
-        nc.scalar.copy(w_wd[:].rearrange("p (t m) -> p t m", t=PACK), w_w[:].rearrange("p (m t) -> p t m", t=PACK))
-        w_sd = deal(w_s, U8, U8, "w_sd", tag="xt_s")
-        late_w = sb.tile([P, N + O + N], U32, name="late_w", tag="w_w", align_bytes=64)
-        ws_w, sx_w, wb_w = late_w[:, 0:N], late_w[:, N:N + O], late_w[:, N + O:]
-        late_s = zeroed(nc.gpsimd, N + O + N, "late_s")
-        ws_s, sx_s, wb_s = late_s[:, 0:N], late_s[:, N:N + O], late_s[:, N + O:]
-        fill_words(nc.sync, ws_w, ws_words)
-        fill_words(nc.sync, sx_w, sx_words)
-        fill_words(nc.sync, wb_w, wb_words)
-        load_scales(nc.sync, ws_s, ws_scales)
-        load_scales(nc.sync, sx_s, sx_scales)
-        load_scales(nc.sync, wb_s, wb_scales)
+        nc.scalar.copy(w_wd[:].rearrange("p (t m) -> p m t", t=PACK), w_w[:].rearrange("p (m t) -> p m t", t=PACK))
+        w_sd = deal_scales(w_s, "w_sd", "xt_s")
         xo_wg = gather(xo_w, l2, U32, J, "xo_wg", tag="w_s")
         xo_sg = gather(xo_s, l2, U8, J, "xo_sg")
-        w2_wd = deal(w2_w, U32, I32, "w2_wd", tag="xo_w")
-        w2_sd = deal(w2_s, U8, U8, "w2_sd", tag="w2_w")
+        w2_wd = sb.tile([P, R], U32, name="w2_wd", tag="xo_w", align_bytes=64)
+        nc.vector.tensor_copy(w2_wd[:].bitcast(I32).rearrange("p (t m) -> p m t", t=PACK),
+                              w2_w[:].bitcast(I32).rearrange("p (m t) -> p m t", t=PACK))
+        w2_sd = deal_scales(w2_s, "w2_sd", "w2_w")
 
         a_ps = [ps.tile([P, J], F32, name="a_ps%d" % t) for t in range(PACK)]
         b_ps = [ps.tile([P, J], F32, name="b_ps%d" % t) for t in range(PACK)]

@@ -98,13 +98,13 @@ def tile_list_twotab_looked_skip_plain_kernel(
         xt_wg = gather(xt_w, l1, U16, J, "xt_wg")
         xt_sg = gather(xt_s, l1, U8, J, "xt_sg")
         w_wd = sb.tile([P, R], U32, name="w_wd", align_bytes=64)
-        nc.scalar.copy(w_wd[:].rearrange("p (t m) -> p m t", t=PACK), w_w[:].rearrange("p (m t) -> p m t", t=PACK))
+        nc.scalar.copy(w_wd[:].rearrange("p (t c i) -> p c t i", t=PACK, i=2), w_w[:].rearrange("p (c i t) -> p c t i", t=PACK, i=2))
         w_sd = deal_scales(w_s, "w_sd", "xt_s")
         xo_wg = gather(xo_w, l2, U32, J, "xo_wg", tag="w_s")
         xo_sg = gather(xo_s, l2, U8, J, "xo_sg")
         w2_wd = sb.tile([P, R], U32, name="w2_wd", tag="xo_w", align_bytes=64)
-        nc.vector.tensor_copy(w2_wd[:].bitcast(I32).rearrange("p (t m) -> p m t", t=PACK),
-                              w2_w[:].bitcast(I32).rearrange("p (m t) -> p m t", t=PACK))
+        nc.vector.tensor_copy(w2_wd[:].bitcast(I32).rearrange("p (t c i) -> p c t i", t=PACK, i=2),
+                              w2_w[:].bitcast(I32).rearrange("p (c i t) -> p c t i", t=PACK, i=2))
         w2_sd = deal_scales(w2_s, "w2_sd", "w2_w")
 
         a_ps = [ps.tile([P, J], F32, name="a_ps%d" % t) for t in range(PACK)]
@@ -128,12 +128,12 @@ def tile_list_twotab_looked_skip_plain_kernel(
                                 rhs=xo_wg[:].bitcast(E5M2), rhs_scale=xo_sg[:], start=True, stop=True)
         b_sb = [sb.tile([P, J], F32, name="b_sb%d" % t) for t in range(PACK)]
         for t in range(PACK):
-            if t < 3:
+            if t < 2:
                 nc.vector.tensor_copy(b_sb[t][:], b_ps[t][:])
             else:
                 nc.scalar.activation(b_sb[t][:], b_ps[t][:], COPY)
         for t in range(PACK):
-            if t < 2:
+            if t < 3:
                 nc.vector.tensor_copy(bg[:, t, :], b_sb[t][:].indirect(l4[:]))
             else:
                 nc.scalar.activation(bg[:, t, :], b_sb[t][:].indirect(l4[:]), COPY)
@@ -146,9 +146,8 @@ def tile_list_twotab_looked_skip_plain_kernel(
                                 rhs=sx_w.bitcast(E5M2), rhs_scale=sx_s, start=True, stop=False)
 
         hid = sb.tile([P, O, PACK], BF16, name="hid", align_bytes=64)
-        for u in range(2):
-            pair = slice(2 * u, 2 * u + 2)
-            nc.vector.tensor_max(hid[:, :, pair], ag[:, pair, :].rearrange("p t o -> p o t"), bg[:, pair, :].rearrange("p t o -> p o t"))
+        nc.vector.tensor_max(hid[:].rearrange("p (c i) t -> p c t i", i=2), ag[:].rearrange("p t (c i) -> p c t i", i=2),
+                             bg[:].rearrange("p t (c i) -> p c t i", i=2))
         h_w = sb.tile([P, O], U32, name="h_w", align_bytes=64)
         h_s = sb.tile([P, O], U8, name="h_s", align_bytes=64)
         nc.vector.quantize_mx(out=h_w[:].bitcast(E5M2), scales=h_s[:], in_=hid[:].rearrange("p o t -> p (o t)"))

@@ -15,8 +15,14 @@ COPY = mybir.ActivationFunctionType.Copy
 
 P = 128
 PACK = 4
+QUADRANT = 32
+SCALE_ROWS = 4
+PAIR = 2
 T, Z, J, R, O, N = 1024, 1024, 256, 512, 128, 256
-FLOPS = 335544320
+MX_ALIGN = 64
+B_COPIES_ON_VECTOR = 2
+B_LOOKUPS_ON_VECTOR = 3
+FLOPS = 2 * 512 * (2 * R * J + 2 * N * O)
 
 
 def tile_list_twotab_looked_skip_plain_kernel(
@@ -29,136 +35,140 @@ def tile_list_twotab_looked_skip_plain_kernel(
         ps = ctx.enter_context(tc.psum_pool(name="ps", bufs=1))
 
         def load_list(src, name):
-            t = sb.tile(list(src.shape), U16, name=name)
-            nc.sync.dma_start(t[:], src)
-            return t
+            offsets = sb.tile(list(src.shape), U16, name=name)
+            nc.sync.dma_start(offsets[:], src)
+            return offsets
 
-        def fill_words(eng, dst, src):
-            eng.dma_start(dst.bitcast(I32), src[0].rearrange("p n t -> p (n t)").bitcast(I32))
+        def load_words(queue, src, columns, name):
+            words = sb.tile([P, columns], U32, name=name, align_bytes=MX_ALIGN)
+            queue.dma_start(words[:].bitcast(I32), src[0].rearrange("p n t -> p (n t)").bitcast(I32))
+            return words
 
-        def load_words(eng, src, cols, name, tag=""):
-            t = sb.tile([P, cols], U32, name=name, tag=tag, align_bytes=64)
-            fill_words(eng, t[:], src)
-            return t
+        def zeroed_scale_tile(columns, name):
+            scales = sb.tile([P, columns], U8, name=name, align_bytes=MX_ALIGN)
+            nc.vector.memset(scales[:].bitcast(I32), 0)
+            return scales
 
-        def zeroed(eng, cols, name, tag=""):
-            t = sb.tile([P, cols], U8, name=name, tag=tag, align_bytes=64)
-            eng.memset(t[:].bitcast(I32), 0)
-            return t
+        def load_scales(scales, src):
+            for q in range(P // QUADRANT):
+                nc.sync.dma_start(
+                    scales[QUADRANT * q:QUADRANT * q + SCALE_ROWS, :].bitcast(I32),
+                    src[0].bitcast(I32)[SCALE_ROWS * q:SCALE_ROWS * (q + 1), :],
+                )
 
-        def load_scales(eng, plane, src):
-            for q in range(4):
-                eng.dma_start(plane[32 * q:32 * q + 4, :].bitcast(I32), src[0].bitcast(I32)[4 * q:4 * q + 4, :])
+        xt_s = zeroed_scale_tile(T, "xt_s")
+        w_s = zeroed_scale_tile(R, "w_s")
+        xo_s = zeroed_scale_tile(Z, "xo_s")
+        w2_s = zeroed_scale_tile(R, "w2_s")
 
-        xt_s = zeroed(nc.vector, T, "xt_s")
-        w_s = zeroed(nc.vector, R, "w_s")
-        xo_s = zeroed(nc.vector, Z, "xo_s")
-        w2_s = zeroed(nc.vector, R, "w2_s")
-
-        l1 = load_list(offs, "l1")
-        xt_w = sb.tile([P, T], U16, name="xt_w", align_bytes=64)
+        idx = load_list(offs, "l1")
+        xt_w = sb.tile([P, T], U16, name="xt_w", align_bytes=MX_ALIGN)
         nc.sync.dma_start(xt_w[:].bitcast(I32), xt_words[0].bitcast(I32))
-        l2 = load_list(offs2, "l2")
-        load_scales(nc.sync, xt_s, xt_scales)
+        idx2 = load_list(offs2, "l2")
+        load_scales(xt_s, xt_scales)
         w_w = load_words(nc.sync, w_words, R, "w_w")
         xo_w = load_words(nc.gpsimd, xo_words, Z, "xo_w")
         w2_w = load_words(nc.gpsimd, w2_words, R, "w2_w")
-        load_scales(nc.sync, w_s, w_scales)
-        load_scales(nc.sync, xo_s, xo_scales)
-        load_scales(nc.sync, w2_s, w2_scales)
-        l3 = load_list(offs3, "l3")
-        l4 = load_list(offs4, "l4")
-        late_s = zeroed(nc.vector, N + O + N, "late_s")
-        ws_s, sx_s, wb_s = late_s[:, 0:N], late_s[:, N:N + O], late_s[:, N + O:]
+        load_scales(w_s, w_scales)
+        load_scales(xo_s, xo_scales)
+        load_scales(w2_s, w2_scales)
+        idx3 = load_list(offs3, "l3")
+        idx4 = load_list(offs4, "l4")
+        last_s = zeroed_scale_tile(N + O + N, "late_s")
+        ws_s, sx_s, wb_s = last_s[:, 0:N], last_s[:, N:N + O], last_s[:, N + O:]
         ws_w = load_words(nc.sync, ws_words, N, "ws_w")
-        sx_w = load_words(nc.sync, sx_words, O, "sx_w")[:]
-        load_scales(nc.sync, ws_s, ws_scales)
-        load_scales(nc.sync, sx_s, sx_scales)
+        sx_w = load_words(nc.sync, sx_words, O, "sx_w")
+        load_scales(ws_s, ws_scales)
+        load_scales(sx_s, sx_scales)
         wb_w = load_words(nc.sync, wb_words, N, "wb_w")
-        load_scales(nc.sync, wb_s, wb_scales)
+        load_scales(wb_s, wb_scales)
 
-        def gather(window, lst, dtype, cols, name, tag=""):
-            t = sb.tile([P, cols], dtype, name=name, tag=tag, align_bytes=64)
-            nc.vector.tensor_copy(t[:], window[:].indirect(lst[:]))
-            return t
+        def gather_packed(window, offsets, dtype, name, tag=""):
+            picked = sb.tile([P, J], dtype, name=name, tag=tag, align_bytes=MX_ALIGN)
+            nc.vector.tensor_copy(picked[:], window[:].indirect(offsets[:]))
+            return picked
 
-        def deal(src, dtype, view, name, tag=""):
-            t = sb.tile([P, R], dtype, name=name, tag=tag, align_bytes=64)
-            nc.vector.tensor_copy(t[:].bitcast(view).rearrange("p (t m) -> p t m", t=PACK),
-                                  src[:].bitcast(view).rearrange("p (m t) -> p t m", t=PACK))
-            return t
-
-        def deal_scales(src, name, tag):
-            dealt = sb.tile([P, R], U8, name=name, tag=tag, align_bytes=64)
-            for u in range(2):
-                nc.vector.tensor_copy(dealt[:].rearrange("p (t m) -> p t m", t=PACK)[:, 2 * u:2 * u + 2, :],
-                                      src[:].rearrange("p (m t) -> p t m", t=PACK)[:, 2 * u:2 * u + 2, :])
+        def deal_words(words, name, tag=""):
+            dealt = sb.tile([P, R], U32, name=name, tag=tag, align_bytes=MX_ALIGN)
+            nc.vector.tensor_copy(
+                dealt[:].bitcast(I32).rearrange("p (t c i) -> p c t i", t=PACK, i=PAIR),
+                words[:].bitcast(I32).rearrange("p (c i t) -> p c t i", t=PACK, i=PAIR),
+            )
             return dealt
 
-        xt_wg = gather(xt_w, l1, U16, J, "xt_wg")
-        xt_sg = gather(xt_s, l1, U8, J, "xt_sg")
-        w_wd = sb.tile([P, R], U32, name="w_wd", align_bytes=64)
-        nc.scalar.copy(w_wd[:].rearrange("p (t c i) -> p c t i", t=PACK, i=2), w_w[:].rearrange("p (c i t) -> p c t i", t=PACK, i=2))
-        w_sd = deal_scales(w_s, "w_sd", "xt_s")
-        xo_wg = gather(xo_w, l2, U32, J, "xo_wg", tag="w_s")
-        xo_sg = gather(xo_s, l2, U8, J, "xo_sg")
-        w2_wd = sb.tile([P, R], U32, name="w2_wd", tag="xo_w", align_bytes=64)
-        nc.vector.tensor_copy(w2_wd[:].bitcast(I32).rearrange("p (t c i) -> p c t i", t=PACK, i=2),
-                              w2_w[:].bitcast(I32).rearrange("p (c i t) -> p c t i", t=PACK, i=2))
-        w2_sd = deal_scales(w2_s, "w2_sd", "w2_w")
+        def deal_scales(scales, name, tag):
+            dealt = sb.tile([P, R], U8, name=name, tag=tag, align_bytes=MX_ALIGN)
+            for half in (slice(0, PACK // 2), slice(PACK // 2, PACK)):
+                nc.vector.tensor_copy(
+                    dealt[:].rearrange("p (t m) -> p t m", t=PACK)[:, half, :],
+                    scales[:].rearrange("p (m t) -> p t m", t=PACK)[:, half, :],
+                )
+            return dealt
+
+        xt_wg = gather_packed(xt_w, idx, U16, "xt_wg")
+        xt_sg = gather_packed(xt_s, idx, U8, "xt_sg")
+        w_wd = deal_words(w_w, "w_wd")
+        w_sd = deal_scales(w_s, "w_sd", tag="xt_s")
+        xo_wg = gather_packed(xo_w, idx2, U32, "xo_wg", tag="w_s")
+        xo_sg = gather_packed(xo_s, idx2, U8, "xo_sg")
+        w2_wd = deal_words(w2_w, "w2_wd", tag="xo_w")
+        w2_sd = deal_scales(w2_s, "w2_sd", tag="w2_w")
 
         a_ps = [ps.tile([P, J], F32, name="a_ps%d" % t) for t in range(PACK)]
         b_ps = [ps.tile([P, J], F32, name="b_ps%d" % t) for t in range(PACK)]
 
-        ag = sb.tile([P, PACK, O], F32, name="ag")
-        bg = sb.tile([P, PACK, O], F32, name="bg")
+        a_picked = sb.tile([P, PACK, O], F32, name="ag")
+        b_picked = sb.tile([P, PACK, O], F32, name="bg")
         for t in range(PACK):
-            cols = slice(t * P, (t + 1) * P)
-            nc.tensor.matmul_mx(out=a_ps[t][:], lhsT=w_wd[:, cols].bitcast(E5M2), lhsT_scale=w_sd[:, cols],
+            rows = slice(t * P, (t + 1) * P)
+            nc.tensor.matmul_mx(out=a_ps[t][:], lhsT=w_wd[:, rows].bitcast(E5M2), lhsT_scale=w_sd[:, rows],
                                 rhs=xt_wg[:].bitcast(E2M1), rhs_scale=xt_sg[:], start=True, stop=True)
         a_sb = [sb.tile([P, J], F32, name="a_sb%d" % t) for t in range(PACK)]
         for t in range(PACK):
             nc.scalar.activation(a_sb[t][:], a_ps[t][:], COPY)
         for t in range(PACK):
-            nc.scalar.activation(ag[:, t, :], a_sb[t][:].indirect(l3[:]), COPY)
+            nc.scalar.activation(a_picked[:, t, :], a_sb[t][:].indirect(idx3[:]), COPY)
 
         for t in range(PACK):
-            cols = slice(t * P, (t + 1) * P)
-            nc.tensor.matmul_mx(out=b_ps[t][:], lhsT=w2_wd[:, cols].bitcast(E4M3), lhsT_scale=w2_sd[:, cols],
+            rows = slice(t * P, (t + 1) * P)
+            nc.tensor.matmul_mx(out=b_ps[t][:], lhsT=w2_wd[:, rows].bitcast(E4M3), lhsT_scale=w2_sd[:, rows],
                                 rhs=xo_wg[:].bitcast(E5M2), rhs_scale=xo_sg[:], start=True, stop=True)
         b_sb = [sb.tile([P, J], F32, name="b_sb%d" % t) for t in range(PACK)]
         for t in range(PACK):
-            if t < 2:
+            if t < B_COPIES_ON_VECTOR:
                 nc.vector.tensor_copy(b_sb[t][:], b_ps[t][:])
             else:
                 nc.scalar.activation(b_sb[t][:], b_ps[t][:], COPY)
         for t in range(PACK):
-            if t < 3:
-                nc.vector.tensor_copy(bg[:, t, :], b_sb[t][:].indirect(l4[:]))
+            if t < B_LOOKUPS_ON_VECTOR:
+                nc.vector.tensor_copy(b_picked[:, t, :], b_sb[t][:].indirect(idx4[:]))
             else:
-                nc.scalar.activation(bg[:, t, :], b_sb[t][:].indirect(l4[:]), COPY)
+                nc.scalar.activation(b_picked[:, t, :], b_sb[t][:].indirect(idx4[:]), COPY)
 
+        y_ps = [ps.tile([P, O], F32, name="y_ps%d" % h, tag="b_ps%d" % h) for h in range(N // P)]
+        for h in range(N // P):
+            rows = slice(h * P, (h + 1) * P)
+            nc.tensor.matmul_mx(out=y_ps[h][:], lhsT=ws_w[:, rows].bitcast(E4M3), lhsT_scale=ws_s[:, rows],
+                                rhs=sx_w[:].bitcast(E5M2), rhs_scale=sx_s, start=True, stop=False)
 
-        y_ps = [ps.tile([P, O], F32, name="y_ps%d" % h, tag="b_ps%d" % h) for h in range(2)]
-        for h in range(2):
-            cols = slice(h * P, (h + 1) * P)
-            nc.tensor.matmul_mx(out=y_ps[h][:], lhsT=ws_w[:, cols].bitcast(E4M3), lhsT_scale=ws_s[:, cols],
-                                rhs=sx_w.bitcast(E5M2), rhs_scale=sx_s, start=True, stop=False)
+        hid = sb.tile([P, O, PACK], BF16, name="hid", align_bytes=MX_ALIGN)
+        nc.vector.tensor_max(
+            hid[:].rearrange("p (c i) t -> p c t i", i=PAIR),
+            a_picked[:].rearrange("p t (c i) -> p c t i", i=PAIR),
+            b_picked[:].rearrange("p t (c i) -> p c t i", i=PAIR),
+        )
+        hid_w = sb.tile([P, O], U32, name="h_w", align_bytes=MX_ALIGN)
+        hid_s = sb.tile([P, O], U8, name="h_s", align_bytes=MX_ALIGN)
+        nc.vector.quantize_mx(out=hid_w[:].bitcast(E5M2), scales=hid_s[:], in_=hid[:].rearrange("p o t -> p (o t)"))
 
-        hid = sb.tile([P, O, PACK], BF16, name="hid", align_bytes=64)
-        nc.vector.tensor_max(hid[:].rearrange("p (c i) t -> p c t i", i=2), ag[:].rearrange("p t (c i) -> p c t i", i=2),
-                             bg[:].rearrange("p t (c i) -> p c t i", i=2))
-        h_w = sb.tile([P, O], U32, name="h_w", align_bytes=64)
-        h_s = sb.tile([P, O], U8, name="h_s", align_bytes=64)
-        nc.vector.quantize_mx(out=h_w[:].bitcast(E5M2), scales=h_s[:], in_=hid[:].rearrange("p o t -> p (o t)"))
+        for h in range(N // P):
+            rows = slice(h * P, (h + 1) * P)
+            nc.tensor.matmul_mx(out=y_ps[h][:], lhsT=wb_w[:, rows].bitcast(E4M3), lhsT_scale=wb_s[:, rows],
+                                rhs=hid_w[:].bitcast(E5M2), rhs_scale=hid_s[:], start=False, stop=True)
 
-        for h in range(2):
-            cols = slice(h * P, (h + 1) * P)
-            nc.tensor.matmul_mx(out=y_ps[h][:], lhsT=wb_w[:, cols].bitcast(E4M3), lhsT_scale=wb_s[:, cols],
-                                rhs=h_w[:].bitcast(E5M2), rhs_scale=h_s[:], start=False, stop=True)
-        y0 = sb.tile([P, O], F32, name="y0")
-        y1 = sb.tile([P, O], F32, name="y1")
-        nc.vector.tensor_copy(y0[:], y_ps[0][:])
-        nc.sync.dma_start(out[0:P, :], y0[:])
-        nc.scalar.activation(y1[:], y_ps[1][:], COPY)
-        nc.scalar.dma_start(out[P:2 * P, :], y1[:])
+        y_low = sb.tile([P, O], F32, name="y0")
+        y_high = sb.tile([P, O], F32, name="y1")
+        nc.vector.tensor_copy(y_low[:], y_ps[0][:])
+        nc.sync.dma_start(out[0:P, :], y_low[:])
+        nc.scalar.activation(y_high[:], y_ps[1][:], COPY)
+        nc.scalar.dma_start(out[P:N, :], y_high[:])

from contextlib import ExitStack

import concourse.mybir as mybir

F32 = mybir.dt.float32
BF16 = mybir.dt.bfloat16
I32 = mybir.dt.int32
U32 = mybir.dt.uint32
U16 = mybir.dt.uint16
U8 = mybir.dt.uint8
E4M3 = mybir.dt.float8_e4m3fn_x4
E5M2 = mybir.dt.float8_e5m2_x4
E2M1 = mybir.dt.float4_e2m1fn_x4
COPY = mybir.ActivationFunctionType.Copy

P = 128
PACK = 4
QUADRANT = 32
SCALE_ROWS = 4
PAIR = 2
T, Z, J, R, O, N = 1024, 1024, 256, 512, 128, 256
MX_ALIGN = 64
B_COPIES_ON_VECTOR = 2
B_LOOKUPS_ON_VECTOR = 3
FLOPS = 2 * 512 * (2 * R * J + 2 * N * O)


def tile_list_twotab_looked_skip_plain_kernel(
    tc, xt_words, xt_scales, w_words, w_scales, xo_words, xo_scales, w2_words, w2_scales,
    wb_words, wb_scales, sx_words, sx_scales, ws_words, ws_scales, offs, offs2, offs3, offs4, out,
):
    nc = tc.nc
    with ExitStack() as ctx:
        sb = ctx.enter_context(tc.tile_pool(name="sb", bufs=1))
        ps = ctx.enter_context(tc.psum_pool(name="ps", bufs=1))

        def load_list(src, name):
            offsets = sb.tile(list(src.shape), U16, name=name)
            nc.sync.dma_start(offsets[:], src)
            return offsets

        def load_words(queue, src, columns, name):
            words = sb.tile([P, columns], U32, name=name, align_bytes=MX_ALIGN)
            queue.dma_start(words[:].bitcast(I32), src[0].rearrange("p n t -> p (n t)").bitcast(I32))
            return words

        def zeroed_scale_tile(columns, name):
            scales = sb.tile([P, columns], U8, name=name, align_bytes=MX_ALIGN)
            nc.vector.memset(scales[:].bitcast(I32), 0)
            return scales

        def load_scales(scales, src):
            for q in range(P // QUADRANT):
                nc.sync.dma_start(
                    scales[QUADRANT * q:QUADRANT * q + SCALE_ROWS, :].bitcast(I32),
                    src[0].bitcast(I32)[SCALE_ROWS * q:SCALE_ROWS * (q + 1), :],
                )

        xt_s = zeroed_scale_tile(T, "xt_s")
        w_s = zeroed_scale_tile(R, "w_s")
        xo_s = zeroed_scale_tile(Z, "xo_s")
        w2_s = zeroed_scale_tile(R, "w2_s")

        idx = load_list(offs, "l1")
        xt_w = sb.tile([P, T], U16, name="xt_w", align_bytes=MX_ALIGN)
        nc.sync.dma_start(xt_w[:].bitcast(I32), xt_words[0].bitcast(I32))
        idx2 = load_list(offs2, "l2")
        load_scales(xt_s, xt_scales)
        w_w = load_words(nc.sync, w_words, R, "w_w")
        xo_w = load_words(nc.gpsimd, xo_words, Z, "xo_w")
        w2_w = load_words(nc.gpsimd, w2_words, R, "w2_w")
        load_scales(w_s, w_scales)
        load_scales(xo_s, xo_scales)
        load_scales(w2_s, w2_scales)
        idx3 = load_list(offs3, "l3")
        idx4 = load_list(offs4, "l4")
        last_s = zeroed_scale_tile(N + O + N, "late_s")
        ws_s, sx_s, wb_s = last_s[:, 0:N], last_s[:, N:N + O], last_s[:, N + O:]
        ws_w = load_words(nc.sync, ws_words, N, "ws_w")
        sx_w = load_words(nc.sync, sx_words, O, "sx_w")
        load_scales(ws_s, ws_scales)
        load_scales(sx_s, sx_scales)
        wb_w = load_words(nc.sync, wb_words, N, "wb_w")
        load_scales(wb_s, wb_scales)

        def gather_packed(window, offsets, dtype, name, tag=""):
            picked = sb.tile([P, J], dtype, name=name, tag=tag, align_bytes=MX_ALIGN)
            nc.vector.tensor_copy(picked[:], window[:].indirect(offsets[:]))
            return picked

        def deal_words(words, name, tag=""):
            dealt = sb.tile([P, R], U32, name=name, tag=tag, align_bytes=MX_ALIGN)
            nc.vector.tensor_copy(
                dealt[:].bitcast(I32).rearrange("p (t c i) -> p c t i", t=PACK, i=PAIR),
                words[:].bitcast(I32).rearrange("p (c i t) -> p c t i", t=PACK, i=PAIR),
            )
            return dealt

        def deal_scales(scales, name, tag):
            dealt = sb.tile([P, R], U8, name=name, tag=tag, align_bytes=MX_ALIGN)
            for half in (slice(0, PACK // 2), slice(PACK // 2, PACK)):
                nc.vector.tensor_copy(
                    dealt[:].rearrange("p (t m) -> p t m", t=PACK)[:, half, :],
                    scales[:].rearrange("p (m t) -> p t m", t=PACK)[:, half, :],
                )
            return dealt

        xt_wg = gather_packed(xt_w, idx, U16, "xt_wg")
        xt_sg = gather_packed(xt_s, idx, U8, "xt_sg")
        w_wd = deal_words(w_w, "w_wd")
        w_sd = deal_scales(w_s, "w_sd", tag="xt_s")
        xo_wg = gather_packed(xo_w, idx2, U32, "xo_wg", tag="w_s")
        xo_sg = gather_packed(xo_s, idx2, U8, "xo_sg")
        w2_wd = deal_words(w2_w, "w2_wd", tag="xo_w")
        w2_sd = deal_scales(w2_s, "w2_sd", tag="w2_w")

        a_ps = [ps.tile([P, J], F32, name="a_ps%d" % t) for t in range(PACK)]
        b_ps = [ps.tile([P, J], F32, name="b_ps%d" % t) for t in range(PACK)]

        a_picked = sb.tile([P, PACK, O], F32, name="ag")
        b_picked = sb.tile([P, PACK, O], F32, name="bg")
        for t in range(PACK):
            rows = slice(t * P, (t + 1) * P)
            nc.tensor.matmul_mx(out=a_ps[t][:], lhsT=w_wd[:, rows].bitcast(E5M2), lhsT_scale=w_sd[:, rows],
                                rhs=xt_wg[:].bitcast(E2M1), rhs_scale=xt_sg[:], start=True, stop=True)
        a_sb = [sb.tile([P, J], F32, name="a_sb%d" % t) for t in range(PACK)]
        for t in range(PACK):
            nc.scalar.activation(a_sb[t][:], a_ps[t][:], COPY)
        for t in range(PACK):
            nc.scalar.activation(a_picked[:, t, :], a_sb[t][:].indirect(idx3[:]), COPY)

        for t in range(PACK):
            rows = slice(t * P, (t + 1) * P)
            nc.tensor.matmul_mx(out=b_ps[t][:], lhsT=w2_wd[:, rows].bitcast(E4M3), lhsT_scale=w2_sd[:, rows],
                                rhs=xo_wg[:].bitcast(E5M2), rhs_scale=xo_sg[:], start=True, stop=True)
        b_sb = [sb.tile([P, J], F32, name="b_sb%d" % t) for t in range(PACK)]
        for t in range(PACK):
            if t < B_COPIES_ON_VECTOR:
                nc.vector.tensor_copy(b_sb[t][:], b_ps[t][:])
            else:
                nc.scalar.activation(b_sb[t][:], b_ps[t][:], COPY)
        for t in range(PACK):
            if t < B_LOOKUPS_ON_VECTOR:
                nc.vector.tensor_copy(b_picked[:, t, :], b_sb[t][:].indirect(idx4[:]))
            else:
                nc.scalar.activation(b_picked[:, t, :], b_sb[t][:].indirect(idx4[:]), COPY)

        y_ps = [ps.tile([P, O], F32, name="y_ps%d" % h, tag="b_ps%d" % h) for h in range(N // P)]
        for h in range(N // P):
            rows = slice(h * P, (h + 1) * P)
            nc.tensor.matmul_mx(out=y_ps[h][:], lhsT=ws_w[:, rows].bitcast(E4M3), lhsT_scale=ws_s[:, rows],
                                rhs=sx_w[:].bitcast(E5M2), rhs_scale=sx_s, start=True, stop=False)

        hid = sb.tile([P, O, PACK], BF16, name="hid", align_bytes=MX_ALIGN)
        nc.vector.tensor_max(
            hid[:].rearrange("p (c i) t -> p c t i", i=PAIR),
            a_picked[:].rearrange("p t (c i) -> p c t i", i=PAIR),
            b_picked[:].rearrange("p t (c i) -> p c t i", i=PAIR),
        )
        hid_w = sb.tile([P, O], U32, name="h_w", align_bytes=MX_ALIGN)
        hid_s = sb.tile([P, O], U8, name="h_s", align_bytes=MX_ALIGN)
        nc.vector.quantize_mx(out=hid_w[:].bitcast(E5M2), scales=hid_s[:], in_=hid[:].rearrange("p o t -> p (o t)"))

        for h in range(N // P):
            rows = slice(h * P, (h + 1) * P)
            nc.tensor.matmul_mx(out=y_ps[h][:], lhsT=wb_w[:, rows].bitcast(E4M3), lhsT_scale=wb_s[:, rows],
                                rhs=hid_w[:].bitcast(E5M2), rhs_scale=hid_s[:], start=False, stop=True)

        y_low = sb.tile([P, O], F32, name="y0")
        y_high = sb.tile([P, O], F32, name="y1")
        nc.vector.tensor_copy(y_low[:], y_ps[0][:])
        nc.sync.dma_start(out[0:P, :], y_low[:])
        nc.scalar.activation(y_high[:], y_ps[1][:], COPY)
        nc.scalar.dma_start(out[P:N, :], y_high[:])
